import numpy as np
import ml_dtypes


def mxq(x, axis, fmt="e4m3"):
    dtype, down = {"e4m3": (ml_dtypes.float8_e4m3fn, 7), "e5m2": (ml_dtypes.float8_e5m2, 14)}[fmt]
    v = np.moveaxis(np.asarray(x, np.float32).astype(ml_dtypes.bfloat16).astype(np.float64), axis, -1)
    blocks = v.reshape(v.shape[:-1] + (-1, 32))
    amax = np.abs(blocks).max(-1, keepdims=True)
    byte = np.maximum(np.where(amax > 0, np.frexp(amax)[1] - 1 + 127, 0) - down, 1)
    scale = np.exp2(byte - 127.0)
    codes = (blocks / scale).astype(np.float32).astype(dtype).astype(np.float64)
    return np.moveaxis((codes * scale).reshape(v.shape), -1, axis)


WIDE = False


def mx_kscale(k):
    if not WIDE:
        return np.ones(k)
    levels = np.array([10, -10, 5, -5, 0])
    if k % 512:
        return np.exp2(np.random.permutation(np.resize(levels, k // 32))).repeat(32)
    a = np.empty((k // 512, 16))
    for p in range(k // 512):
        a[p, :8] = np.random.permutation(np.resize(levels, 8))
        for g in range(8):
            far = levels[np.abs(levels - a[p, g]) >= 10]
            a[p, g + 8] = far[np.random.randint(len(far))]
    return np.exp2(a.ravel()).repeat(32)


def f64(x):
    return np.asarray(x).astype(np.float64)


def striped(idx):
    return np.tile(idx.reshape(-1, 16).T, (8, 1)).astype(np.uint16)


def unstriped(offs):
    return offs[:16].T.reshape(-1).astype(np.int64)


def pack_weight(w):
    k, n = w.shape
    w = f64(np.asarray(w, np.float32).astype(ml_dtypes.bfloat16)).reshape(k // 32, 32, n)
    amax = np.abs(w).max(1)
    byte = np.clip(np.where(amax > 0, np.frexp(amax)[1] - 1 + 127 - 7, 1), 1, 254)
    scaled = (w * np.exp2(127.0 - byte)[:, None, :]).reshape(k, n).astype(np.float32)
    words = np.ascontiguousarray(scaled.reshape(k // 512, 128, 4, n).transpose(0, 1, 3, 2)).astype(ml_dtypes.float8_e4m3fn).view(np.uint8)
    return words, np.ascontiguousarray(byte.astype(np.uint8).reshape(k // 512, 16, n))


def unpack_weight(words, scales):
    g, p, n, _ = words.shape
    vals = np.ascontiguousarray(words).view(ml_dtypes.float8_e4m3fn).astype(np.float64) * np.repeat(np.exp2(scales.astype(np.float64) - 127.0), 8, axis=1)[..., None]
    return vals.transpose(0, 1, 3, 2).reshape(g * 512, n)


K, T, S, D, N = 1024, 2048, 512, 4, 256
P = 2 ** 7


def setup_inputs():
    n = np.random.standard_normal
    s = mx_kscale(K)[:, None]
    packed_xT = pack_weight(n((K, T)) * s)
    return {
        "x_words": packed_xT[0],
        "x_scales": packed_xT[1],
        "w1": (n((K, N)) / np.sqrt(K) / s).astype(np.float32),
        "w2": (n((K, N)) / np.sqrt(K) / s).astype(np.float32),
        "cot": (np.tile(np.random.uniform(0.2, 1.0, S), (P, 1))).astype(np.float32),
        "rx": (np.tile(n(S), (P, 1))).astype(np.float32),
        "ry": (np.tile(n(S), (P, 1))).astype(np.float32),
        "offs": striped(np.random.permutation(T)[:S]),
    }


def reference(x_words, x_scales, w1, w2, cot, rx, ry, offs):
    xq = unpack_weight(x_words, x_scales)[:, unstriped(offs)]
    y = mxq(f64(w1), 0, "e4m3").T @ xq
    z = mxq(f64(w2), 0, "e4m3").T @ xq
    da = f64(cot)[:1] * (f64(rx)[:1] * y + f64(ry)[:1] * z)
    aa = da.reshape(len(da), -1, D).sum(axis=2)
    ds = f64(cot)[:1] * (f64(rx)[:1] * z - (f64(ry)[:1] * y))
    ss = ds.reshape(len(ds), -1, D).sum(axis=2)
    nn = np.sqrt((aa) ** 2 + (ss) ** 2 + 0.1)
    cs = aa / nn
    sn = ss / nn
    rt = np.repeat(cs, D, axis=1) * f64(rx)[:1] - (np.repeat(sn, D, axis=1) * f64(ry)[:1])
    wr = f64(cot)[:1] * rt
    return wr.reshape(len(wr), -1, D).sum(axis=2)

@@ -1,0 +1,205 @@
+from contextlib import ExitStack
+
+import concourse.mybir as mybir
+from concourse.masks import make_identity
+
+K, T, S, D, N = 1024, 2048, 512, 4, 256
+FLOPS = 2 * 2 * K * N * S
+
+F32 = mybir.dt.float32
+BF16 = mybir.dt.bfloat16
+I32 = mybir.dt.int32
+U32 = mybir.dt.uint32
+U16 = mybir.dt.uint16
+U8 = mybir.dt.uint8
+FP8X4 = mybir.dt.float8_e4m3fn_x4
+ACT = mybir.ActivationFunctionType
+ALU = mybir.AluOpType
+
+P = 128
+PACK = 4
+PASSES = K // (P * PACK)
+V = S // D
+BLOCKS = N // P
+SPLIT = 168
+
+
+def tile_picked_yarap_rhs_p_kernel(
+    tc, x_words, x_scales, w1, w2, cot, rx, ry, offs, out
+):
+    nc = tc.nc
+    with ExitStack() as ctx:
+        sb = ctx.enter_context(tc.tile_pool(name="sb", bufs=1))
+        ps = ctx.enter_context(tc.psum_pool(name="ps", bufs=1))
+
+        offsets = sb.tile([P, S // 16], U16, name="offsets")
+        x_table = [sb.tile([P, T], U32, name=f"x_table{o}", align_bytes=64) for o in range(PASSES)]
+        s_table = sb.tile([P, T], U8, name="s_table")
+        w_raw = {(c, o): sb.tile([P, PACK, N], F32, name=f"w_raw{c}{o}", align_bytes=64) for c in range(2) for o in range(PASSES)}
+        w_bf = {}
+        w_codes = {(c, o): sb.tile([P, N], U32, name=f"w_codes{c}{o}", align_bytes=64) for c in range(2) for o in range(PASSES)}
+        w_scales = {(c, o): sb.tile([P, N], U8, name=f"w_scales{c}{o}", align_bytes=64) for c in range(2) for o in range(PASSES)}
+        x_codes = [sb.tile([P, S], U32, name="x_codes0", align_bytes=64)]
+        s_picked = sb.tile([P, S], U8, name="s_picked", align_bytes=64)
+        s_dealt = sb.tile([P, S], U8, name="s_dealt", align_bytes=64)
+        ident = sb.tile([P, P], F32, name="ident")
+        cot_t = sb.tile([P, D], F32, name="cot_t")
+        rest = sb.tile([P, 2, 8], F32, name="rest")
+
+        def load_x(o):
+            nc.sync.dma_start(out=x_table[o][:].bitcast(I32), in_=x_words[o].rearrange("p n t -> p (n t)").bitcast(I32))
+
+        def load_w(c, o):
+            rows = (w1, w2)[c][o * P * PACK : (o + 1) * P * PACK, :]
+            nc.sync.dma_start(out=w_raw[c, o][:], in_=rows.rearrange("(p t) m -> p t m", t=PACK))
+
+        nc.vector.memset(s_table[:].bitcast(I32), 0)
+        nc.sync.dma_start(offsets[:], offs)
+        load_x(0)
+        for q in range(4):
+            nc.sync.dma_start(
+                out=s_table[32 * q : 32 * q + 4 * PASSES, :].bitcast(I32),
+                in_=x_scales[:, 4 * q : 4 * q + 4, :].bitcast(I32),
+            )
+        load_w(0, 0)
+        load_x(1)
+        for dst, row in ((cot_t[:], cot), (rest[:, 0, 0:D], rx), (rest[:, 1, 0:D], ry)):
+            nc.sync.dma_start(out=dst, in_=row[0].rearrange("(v d) -> v d", d=D))
+        load_w(1, 0)
+        load_w(0, 1)
+        load_w(1, 1)
+        make_identity(nc, ident[:])
+
+        warm = sb.tile([P, 1], F32, name="warm")
+        nc.scalar.activation(warm[:], ident[:, 0:1], ACT.Abs_reciprocal_sqrt, bias=0.1)
+
+        acc = [ps.tile([P, 2, V], F32, name=f"acc{h}") for h in range(BLOCKS)]
+        y_bank = [ps.tile([P, 2, N], F32, name=f"y_bank{i}") for i in range(2)]
+        z_bank = [ps.tile([P, N], F32, name=f"z_bank{d}") for d in range(D)]
+
+        def gather_words(o):
+            nc.vector.tensor_copy(
+                x_codes[o][:].rearrange("p (d v) -> p v d", d=D), x_table[o][:].indirect(offsets[:])
+            )
+
+        def cast(c, o, copy, lo=0, hi=N):
+            copy(
+                w_bf[c, o][:, lo:hi, :].rearrange("p (g i) t -> p g t i", i=4),
+                w_raw[c, o][:, :, lo:hi].rearrange("p t (g i) -> p g t i", i=4),
+            )
+
+        def cast_shared(c, o, tag):
+            w_bf[c, o] = sb.tile([P, N, PACK], BF16, name=f"w_bf{c}{o}", tag=tag, align_bytes=64)
+            cast(c, o, nc.vector.tensor_copy, 0, SPLIT)
+            cast(c, o, nc.scalar.copy, SPLIT, N)
+
+        def quantise(c, o):
+            nc.vector.quantize_mx(
+                out=w_codes[c, o][:].bitcast(FP8X4),
+                scales=w_scales[c, o][:],
+                in_=w_bf[c, o][:].rearrange("p m t -> p (m t)"),
+            )
+
+        def product(dst, c, o, d, start, stop):
+            cols = slice(d * V, (d + 1) * V)
+            nc.tensor.matmul_mx(
+                out=dst,
+                lhsT=x_codes[o][:, cols].bitcast(FP8X4),
+                lhsT_scale=s_dealt[4 * o :, cols],
+                rhs=w_codes[c, o][:].bitcast(FP8X4),
+                rhs_scale=w_scales[c, o][:],
+                start=start,
+                stop=stop,
+            )
+
+        gather_words(0)
+        nc.vector.tensor_copy(s_picked[:], s_table[:].indirect(offsets[:]))
+        nc.vector.tensor_copy(
+            s_dealt[:].rearrange("p (d g i) -> p g d i", d=D, i=16),
+            s_picked[:].rearrange("p (g i d) -> p g d i", d=D, i=16),
+        )
+        w_bf[0, 0] = sb.tile([P, N, PACK], BF16, name="w_bf00", align_bytes=64)
+        cast(0, 0, nc.scalar.copy)
+        quantise(0, 0)
+        for d in range(D):
+            product(y_bank[d // 2][:, d % 2, :], 0, 0, d, d % 2 == 0, False)
+        x_codes.append(sb.tile([P, S], U32, name="x_codes1", tag="w_bf00", align_bytes=64))
+        gather_words(1)
+        coef3 = sb.tile([P, 3, D], F32, name="coef3")
+        pairs = sb.tile([P, 2, 2], F32, name="pairs")
+        sums = sb.tile([P, 2], F32, name="sums", tag="w_scales00", align_bytes=64)
+        a, b, nb = coef3[:, 0, :], coef3[:, 1, :], coef3[:, 2, :]
+        nc.gpsimd.tensor_tensor(coef3[:, 0:2, :], rest[:, :, 0:D], cot_t[:].unsqueeze(1).to_broadcast([P, 2, D]), ALU.mult)
+        nc.gpsimd.tensor_scalar(nb, b, -1.0, 0.0, ALU.mult, ALU.add)
+        nc.gpsimd.tensor_tensor(pairs[:], coef3[:, 0:3:2, 0:2], coef3[:, 0:3:2, 2:4], ALU.add)
+        nc.gpsimd.tensor_tensor(sums[:], pairs[:, :, 0], pairs[:, :, 1], ALU.add)
+        for i in range(2):
+            nc.tensor.transpose(acc[0][:, i, :], sums[:, i : i + 1].to_broadcast([P, P]), ident[:])
+        cast_shared(1, 0, "x_table1")
+        quantise(1, 0)
+        for d in range(D):
+            product(z_bank[d][:], 1, 0, d, True, False)
+        cast_shared(0, 1, "w_raw10")
+        spread_t = sb.tile([P, 2, V], F32, name="spread", tag="x_table1", align_bytes=64)
+        spread = spread_t[:]
+        nc.scalar.copy(spread, acc[0][:])
+        quantise(0, 1)
+        for d in range(D):
+            product(y_bank[d // 2][:, d % 2, :], 0, 1, d, False, d % 2 == 1)
+        cast_shared(1, 1, "w_raw01")
+        quantise(1, 1)
+        for d in range(D):
+            product(z_bank[d][:], 1, 1, d, False, True)
+
+        terms_left = [10, 10]
+
+        def add_term(term):
+            for i in range(2):
+                add_half(term[:, i, :], i)
+
+        def add_half(half, i):
+            for h in range(BLOCKS):
+                nc.tensor.matmul(
+                    acc[h][:, i, :], half[:, h * P : (h + 1) * P], ident[:], is_transpose=True,
+                    start=(terms_left[h] == 10), stop=(terms_left[h] == 1),
+                )
+                terms_left[h] = terms_left[h] - 1
+
+        y_terms = [sb.tile([P, 2, N], F32, name=f"y_term{d}") for d in range(D)]
+        z_terms = [sb.tile([P, 2, N], F32, name=f"z_term{d}") for d in range(D)]
+        for d in range(D):
+            y = y_bank[d // 2][:, d % 2, :]
+            for i, coef in enumerate((a, nb)):
+                if d < 3:
+                    nc.scalar.activation(y_terms[d][:, i, :], y, ACT.Copy, scale=coef[:, d : d + 1])
+                else:
+                    nc.vector.tensor_scalar(y_terms[d][:, i, :], y, coef[:, d : d + 1], None, ALU.mult)
+        add_term(y_terms[3])
+        for d in range(D):
+            for i, coef in enumerate((b, a)):
+                if d == 3:
+                    nc.scalar.activation(z_terms[d][:, i, :], z_bank[d][:], ACT.Copy, scale=coef[:, d : d + 1])
+                else:
+                    nc.vector.scalar_tensor_tensor(
+                        z_terms[d][:, i, :], z_bank[d][:], coef[:, d : d + 1], y_terms[d][:, i, :], ALU.mult, ALU.add
+                    )
+        for d in (0, 1, 3, 2):
+            add_term(z_terms[d])
+
+        squares = [sb.tile([P, 2, V], F32, name=f"squares{h}") for h in range(BLOCKS)]
+        scaled = sb.tile([P, 2, BLOCKS, V], F32, name="scaled")
+        norm2 = [sb.tile([P, V], F32, name=f"norm2{h}") for h in range(BLOCKS)]
+        num = sb.tile([P, BLOCKS, V], F32, name="num")
+        inv = [sb.tile([P, V], F32, name=f"inv{h}") for h in range(BLOCKS)]
+        res = [sb.tile([P, V], F32, name=f"res{h}") for h in range(BLOCKS)]
+        nc.scalar.activation(squares[0][:], acc[0][:], ACT.Square)
+        nc.vector.tensor_tensor(scaled[:, :, 1, :], acc[1][:], spread, ALU.mult)
+        nc.scalar.activation(squares[1][:], acc[1][:], ACT.Square)
+        nc.vector.tensor_tensor(scaled[:, :, 0, :], acc[0][:], spread, ALU.mult)
+        for h in range(BLOCKS):
+            nc.vector.tensor_tensor(norm2[h][:], squares[h][:, 0, :], squares[h][:, 1, :], ALU.add)
+            nc.scalar.activation(inv[h][:], norm2[h][:], ACT.Abs_reciprocal_sqrt, bias=0.1)
+        nc.vector.tensor_tensor(num[:], scaled[:, 0], scaled[:, 1], ALU.add)
+        for h in range(BLOCKS):
+            nc.vector.tensor_tensor(res[h][:], num[:, h, :], inv[h][:], ALU.mult)
+            nc.sync.dma_start(out=out[h * P : (h + 1) * P, :], in_=res[h][:])

@@ -21,13 +21,13 @@ PACK = 4
 PASSES = K // (P * PACK)
 V = S // D
 BLOCKS = N // P
-SPLIT = 168
 
 
 def tile_picked_yarap_rhs_p_kernel(
     tc, x_words, x_scales, w1, w2, cot, rx, ry, offs, out
 ):
     nc = tc.nc
+    weights = (w1, w2)
     with ExitStack() as ctx:
         sb = ctx.enter_context(tc.tile_pool(name="sb", bufs=1))
         ps = ctx.enter_context(tc.psum_pool(name="ps", bufs=1))
@@ -35,11 +35,13 @@ def tile_picked_yarap_rhs_p_kernel(
         offsets = sb.tile([P, S // 16], U16, name="offsets")
         x_table = [sb.tile([P, T], U32, name=f"x_table{o}", align_bytes=64) for o in range(PASSES)]
         s_table = sb.tile([P, T], U8, name="s_table")
-        w_raw = {(c, o): sb.tile([P, PACK, N], F32, name=f"w_raw{c}{o}", align_bytes=64) for c in range(2) for o in range(PASSES)}
+        raw0 = [sb.tile([P, PACK, N], F32, name=f"raw0_{c}", align_bytes=64) for c in range(2)]
+        raw1 = {(h, c): sb.tile([P, PACK, P], F32, name=f"raw1_{h}{c}", align_bytes=64) for h in range(BLOCKS) for c in range(2)}
+        w_codes = {(o, h): sb.tile([P, 2 * P], U32, name=f"w_codes{o}{h}", align_bytes=64) for o in range(PASSES) for h in range(BLOCKS)}
+        w_scales = {(o, h): sb.tile([P, 2 * P], U8, name=f"w_scales{o}{h}", align_bytes=64) for o in range(PASSES) for h in range(BLOCKS)}
         w_bf = {}
-        w_codes = {(c, o): sb.tile([P, N], U32, name=f"w_codes{c}{o}", align_bytes=64) for c in range(2) for o in range(PASSES)}
-        w_scales = {(c, o): sb.tile([P, N], U8, name=f"w_scales{c}{o}", align_bytes=64) for c in range(2) for o in range(PASSES)}
-        x_codes = [sb.tile([P, S], U32, name="x_codes0", align_bytes=64)]
+        x_codes = [sb.tile([P, S], U32, name=f"x_codes{o}", align_bytes=64) for o in range(PASSES)]
+        x_picked = []
         s_picked = sb.tile([P, S], U8, name="s_picked", align_bytes=64)
         s_dealt = sb.tile([P, S], U8, name="s_dealt", align_bytes=64)
         ident = sb.tile([P, P], F32, name="ident")
@@ -49,9 +51,13 @@ def tile_picked_yarap_rhs_p_kernel(
         def load_x(o):
             nc.sync.dma_start(out=x_table[o][:].bitcast(I32), in_=x_words[o].rearrange("p n t -> p (n t)").bitcast(I32))
 
-        def load_w(c, o):
-            rows = (w1, w2)[c][o * P * PACK : (o + 1) * P * PACK, :]
-            nc.sync.dma_start(out=w_raw[c, o][:], in_=rows.rearrange("(p t) m -> p t m", t=PACK))
+        def load_w(dst, c, o, cols):
+            rows = weights[c][o * P * PACK : (o + 1) * P * PACK, cols]
+            nc.sync.dma_start(out=dst[:], in_=rows.rearrange("(p t) m -> p t m", t=PACK))
+
+        def load_small():
+            for dst, row in ((cot_t[:], cot), (rest[:, 0, 0:D], rx), (rest[:, 1, 0:D], ry)):
+                nc.sync.dma_start(out=dst, in_=row[0].rearrange("(v d) -> v d", d=D))
 
         nc.vector.memset(s_table[:].bitcast(I32), 0)
         nc.sync.dma_start(offsets[:], offs)
@@ -61,145 +67,160 @@ def tile_picked_yarap_rhs_p_kernel(
                 out=s_table[32 * q : 32 * q + 4 * PASSES, :].bitcast(I32),
                 in_=x_scales[:, 4 * q : 4 * q + 4, :].bitcast(I32),
             )
-        load_w(0, 0)
+        for c in range(2):
+            load_w(raw0[c], c, 0, slice(0, N))
+        load_small()
         load_x(1)
-        for dst, row in ((cot_t[:], cot), (rest[:, 0, 0:D], rx), (rest[:, 1, 0:D], ry)):
-            nc.sync.dma_start(out=dst, in_=row[0].rearrange("(v d) -> v d", d=D))
-        load_w(1, 0)
-        load_w(0, 1)
-        load_w(1, 1)
+        for h in range(BLOCKS):
+            for c in range(2):
+                load_w(raw1[h, c], c, 1, slice(h * P, (h + 1) * P))
         make_identity(nc, ident[:])
 
         warm = sb.tile([P, 1], F32, name="warm")
         nc.scalar.activation(warm[:], ident[:, 0:1], ACT.Abs_reciprocal_sqrt, bias=0.1)
 
-        acc = [ps.tile([P, 2, V], F32, name=f"acc{h}") for h in range(BLOCKS)]
-        y_bank = [ps.tile([P, 2, N], F32, name=f"y_bank{i}") for i in range(2)]
-        z_bank = [ps.tile([P, N], F32, name=f"z_bank{d}") for d in range(D)]
+        acc0 = ps.tile([P, 2, V], F32, name="acc0")
+        acc1 = [ps.tile([P, V], F32, name=f"acc1{i}") for i in range(2)]
+        acc = {(0, 0): acc0[:, 0], (0, 1): acc0[:, 1], (1, 0): acc1[0][:], (1, 1): acc1[1][:]}
+        yz_bank = {(h, e): ps.tile([P, 2, 2, P], F32, name=f"yz_bank{h}{e}") for h in range(BLOCKS) for e in range(2)}
+        spread_ps = ps.tile([P, 2, V], F32, name="spread_ps")
+        yz_of = {(h, d): yz_bank[h, d % 2][:, d // 2] for h in range(BLOCKS) for d in range(D)}
+        alone = ((1, 1), (1, 3))
 
         def gather_words(o):
+            nc.vector.tensor_copy(x_picked[o][:], x_table[o][:].indirect(offsets[:]))
+
+        def deal(dst, src, run):
             nc.vector.tensor_copy(
-                x_codes[o][:].rearrange("p (d v) -> p v d", d=D), x_table[o][:].indirect(offsets[:])
+                dst[:].rearrange("p (d g i) -> p g d i", d=D, i=run),
+                src[:].rearrange("p (g i d) -> p g d i", d=D, i=run),
             )
 
-        def cast(c, o, copy, lo=0, hi=N):
+        def cast(o, h, c, copy):
+            src = raw0[c][:, :, h * P : (h + 1) * P] if o == 0 else raw1[h, c][:]
             copy(
-                w_bf[c, o][:, lo:hi, :].rearrange("p (g i) t -> p g t i", i=4),
-                w_raw[c, o][:, :, lo:hi].rearrange("p t (g i) -> p g t i", i=4),
+                w_bf[o, h][:, c].rearrange("p (g i) t -> p g t i", i=4),
+                src.rearrange("p t (g i) -> p g t i", i=4),
             )
 
-        def cast_shared(c, o, tag):
-            w_bf[c, o] = sb.tile([P, N, PACK], BF16, name=f"w_bf{c}{o}", tag=tag, align_bytes=64)
-            cast(c, o, nc.vector.tensor_copy, 0, SPLIT)
-            cast(c, o, nc.scalar.copy, SPLIT, N)
-
-        def quantise(c, o):
+        def quantise(o, h):
             nc.vector.quantize_mx(
-                out=w_codes[c, o][:].bitcast(FP8X4),
-                scales=w_scales[c, o][:],
-                in_=w_bf[c, o][:].rearrange("p m t -> p (m t)"),
+                out=w_codes[o, h][:].bitcast(FP8X4),
+                scales=w_scales[o, h][:],
+                in_=w_bf[o, h][:].rearrange("p c m t -> p (c m t)"),
             )
 
-        def product(dst, c, o, d, start, stop):
-            cols = slice(d * V, (d + 1) * V)
-            nc.tensor.matmul_mx(
-                out=dst,
-                lhsT=x_codes[o][:, cols].bitcast(FP8X4),
-                lhsT_scale=s_dealt[4 * o :, cols],
-                rhs=w_codes[c, o][:].bitcast(FP8X4),
-                rhs_scale=w_scales[c, o][:],
-                start=start,
-                stop=stop,
-            )
+        def products(o, h):
+            for e in range(2):
+                for f in range(2):
+                    d = 2 * f + e
+                    cols = slice(d * V, (d + 1) * V)
+                    nc.tensor.matmul_mx(
+                        out=yz_of[h, d].rearrange("p c m -> p (c m)"),
+                        lhsT=x_codes[o][:, cols].bitcast(FP8X4),
+                        lhsT_scale=s_dealt[4 * o :, cols],
+                        rhs=w_codes[o, h][:].bitcast(FP8X4),
+                        rhs_scale=w_scales[o, h][:],
+                        start=(o == 0 and (f == 0 or (h, d) in alone)),
+                        stop=(o == PASSES - 1 and (f == 1 or (h, d) in alone)),
+                    )
 
+        def bf_tile(o, h, tag=""):
+            w_bf[o, h] = sb.tile([P, 2, P, PACK], BF16, name=f"w_bf{o}{h}", tag=tag or f"w_bf{o}{h}", align_bytes=64)
+
+        x_picked.append(sb.tile([P, S], U32, name="x_picked0", align_bytes=64))
         gather_words(0)
         nc.vector.tensor_copy(s_picked[:], s_table[:].indirect(offsets[:]))
-        nc.vector.tensor_copy(
-            s_dealt[:].rearrange("p (d g i) -> p g d i", d=D, i=16),
-            s_picked[:].rearrange("p (g i d) -> p g d i", d=D, i=16),
-        )
-        w_bf[0, 0] = sb.tile([P, N, PACK], BF16, name="w_bf00", align_bytes=64)
-        cast(0, 0, nc.scalar.copy)
-        quantise(0, 0)
-        for d in range(D):
-            product(y_bank[d // 2][:, d % 2, :], 0, 0, d, d % 2 == 0, False)
-        x_codes.append(sb.tile([P, S], U32, name="x_codes1", tag="w_bf00", align_bytes=64))
-        gather_words(1)
-        coef3 = sb.tile([P, 3, D], F32, name="coef3")
-        pairs = sb.tile([P, 2, 2], F32, name="pairs")
-        sums = sb.tile([P, 2], F32, name="sums", tag="w_scales00", align_bytes=64)
-        a, b, nb = coef3[:, 0, :], coef3[:, 1, :], coef3[:, 2, :]
-        nc.gpsimd.tensor_tensor(coef3[:, 0:2, :], rest[:, :, 0:D], cot_t[:].unsqueeze(1).to_broadcast([P, 2, D]), ALU.mult)
-        nc.gpsimd.tensor_scalar(nb, b, -1.0, 0.0, ALU.mult, ALU.add)
-        nc.gpsimd.tensor_tensor(pairs[:], coef3[:, 0:3:2, 0:2], coef3[:, 0:3:2, 2:4], ALU.add)
-        nc.gpsimd.tensor_tensor(sums[:], pairs[:, :, 0], pairs[:, :, 1], ALU.add)
-        for i in range(2):
-            nc.tensor.transpose(acc[0][:, i, :], sums[:, i : i + 1].to_broadcast([P, P]), ident[:])
-        cast_shared(1, 0, "x_table1")
-        quantise(1, 0)
-        for d in range(D):
-            product(z_bank[d][:], 1, 0, d, True, False)
-        cast_shared(0, 1, "w_raw10")
-        spread_t = sb.tile([P, 2, V], F32, name="spread", tag="x_table1", align_bytes=64)
-        spread = spread_t[:]
-        nc.scalar.copy(spread, acc[0][:])
-        quantise(0, 1)
-        for d in range(D):
-            product(y_bank[d // 2][:, d % 2, :], 0, 1, d, False, d % 2 == 1)
-        cast_shared(1, 1, "w_raw01")
-        quantise(1, 1)
-        for d in range(D):
-            product(z_bank[d][:], 1, 1, d, False, True)
-
-        terms_left = [10, 10]
-
-        def add_term(term):
-            for i in range(2):
-                add_half(term[:, i, :], i)
-
-        def add_half(half, i):
+        deal(x_codes[0], x_picked[0], 4)
+        deal(s_dealt, s_picked, 16)
+        for h in range(BLOCKS):
+            bf_tile(0, h)
+        for c in range(2):
             for h in range(BLOCKS):
-                nc.tensor.matmul(
-                    acc[h][:, i, :], half[:, h * P : (h + 1) * P], ident[:], is_transpose=True,
-                    start=(terms_left[h] == 10), stop=(terms_left[h] == 1),
-                )
-                terms_left[h] = terms_left[h] - 1
+                cast(0, h, c, nc.scalar.copy)
+        for h in range(BLOCKS):
+            quantise(0, h)
+        products(0, 0)
+        coef3 = sb.tile([P, 4, D], F32, name="coef3", tag="raw0_1", align_bytes=64)
+        sums = sb.tile([P, 2], F32, name="sums")
+        a, b, nb = coef3[:, 0, :], coef3[:, 1, :], coef3[:, 2, :]
+        for d in range(D):
+            nc.scalar.activation(coef3[:, 0:2, d], rest[:, :, d], ACT.Copy, scale=cot_t[:, d : d + 1])
+        nc.scalar.activation(coef3[:, 3, :], a, ACT.Copy, accum_out=sums[:, 0:1])
+        nc.scalar.activation(nb, b, ACT.Copy, scale=-1.0, accum_out=sums[:, 1:2])
+        for i in range(2):
+            nc.tensor.transpose(spread_ps[:, i, :], sums[:, i : i + 1].to_broadcast([P, P]), ident[:])
+        spread = sb.tile([P, 2, V], F32, name="spread")
+        nc.scalar.copy(spread[:], spread_ps[:])
+        last_bank = ps.tile([P, 2, P], F32, name="last_bank", tag="spread_ps")
+        yz_of[1, 3] = last_bank[:]
+        products(0, 1)
+        x_picked.append(sb.tile([P, S], U32, name="x_picked1", tag="w_bf01", align_bytes=64))
+        gather_words(1)
 
-        y_terms = [sb.tile([P, 2, N], F32, name=f"y_term{d}") for d in range(D)]
-        z_terms = [sb.tile([P, 2, N], F32, name=f"z_term{d}") for d in range(D)]
-        for d in range(D):
-            y = y_bank[d // 2][:, d % 2, :]
-            for i, coef in enumerate((a, nb)):
-                if d < 3:
-                    nc.scalar.activation(y_terms[d][:, i, :], y, ACT.Copy, scale=coef[:, d : d + 1])
+        bf_tile(1, 0, "x_table1")
+        cast(1, 0, 0, nc.scalar.copy)
+        cast(1, 0, 1, nc.vector.tensor_copy)
+        deal(x_codes[1], x_picked[1], 4)
+        quantise(1, 0)
+        products(1, 0)
+        bf_tile(1, 1, "raw1_00")
+        cast(1, 1, 0, nc.scalar.copy)
+        cast(1, 1, 1, nc.vector.tensor_copy)
+        for c in range(2):
+            nc.vector.quantize_mx(
+                out=w_codes[1, 1][:, c * P : (c + 1) * P].bitcast(FP8X4),
+                scales=w_scales[1, 1][:, c * P : (c + 1) * P],
+                in_=w_bf[1, 1][:, c].rearrange("p m t -> p (m t)"),
+            )
+        products(1, 1)
+
+        def add_terms(h, terms):
+            for n, (i, term) in enumerate(terms):
+                mine = [m for m, (j, other) in enumerate(terms) if h == 0 or j == i]
+                nc.tensor.matmul(acc[h, i], term, ident[:], is_transpose=True, start=(n == mine[0]), stop=(n == mine[-1]))
+
+        for h in range(BLOCKS):
+            terms = []
+            for f in range(2):
+                d, e = 2 * f, 2 * f + 1
+                own = [sb.tile([P, 2, P], F32, name=f"own{h}{f}{n}") for n in range(2)]
+                both = [sb.tile([P, 2, P], F32, name=f"both{h}{f}{n}") for n in range(2)]
+                yz = yz_of[h, e]
+                if (h, e) == (1, 3):
+                    nc.scalar.activation(own[1][:], yz_of[h, d], ACT.Copy, scale=b[:, d : d + 1])
+                    nc.scalar.activation(both[0][:], yz, ACT.Copy, scale=a[:, e : e + 1])
+                    nc.scalar.activation(own[0][:], yz_of[h, d], ACT.Copy, scale=a[:, d : d + 1])
+                    terms.extend([(0, both[0][:, 0]), (1, both[0][:, 1]), (0, own[0][:, 0]), (1, own[0][:, 1])])
                 else:
-                    nc.vector.tensor_scalar(y_terms[d][:, i, :], y, coef[:, d : d + 1], None, ALU.mult)
-        add_term(y_terms[3])
-        for d in range(D):
-            for i, coef in enumerate((b, a)):
-                if d == 3:
-                    nc.scalar.activation(z_terms[d][:, i, :], z_bank[d][:], ACT.Copy, scale=coef[:, d : d + 1])
-                else:
-                    nc.vector.scalar_tensor_tensor(
-                        z_terms[d][:, i, :], z_bank[d][:], coef[:, d : d + 1], y_terms[d][:, i, :], ALU.mult, ALU.add
-                    )
-        for d in (0, 1, 3, 2):
-            add_term(z_terms[d])
+                    for n, coef in enumerate((a, b)):
+                        nc.scalar.activation(own[n][:], yz_of[h, d], ACT.Copy, scale=coef[:, d : d + 1])
+                    nc.vector.scalar_tensor_tensor(both[0][:], yz, a[:, e : e + 1], own[0][:], ALU.mult, ALU.add)
+                    terms.extend([(0, both[0][:, 0]), (1, both[0][:, 1])])
+                nc.vector.scalar_tensor_tensor(both[1][:, 0], yz[:, 1], b[:, e : e + 1], own[1][:, 1], ALU.mult, ALU.add)
+                nc.vector.scalar_tensor_tensor(both[1][:, 1], yz[:, 0], nb[:, e : e + 1], own[1][:, 0], ALU.mult, ALU.subtract)
+                terms.extend([(0, both[1][:, 0]), (1, both[1][:, 1])])
+            add_terms(h, terms)
 
         squares = [sb.tile([P, 2, V], F32, name=f"squares{h}") for h in range(BLOCKS)]
-        scaled = sb.tile([P, 2, BLOCKS, V], F32, name="scaled")
+        scaled = [sb.tile([P, 2, V], F32, name=f"scaled{h}") for h in range(BLOCKS)]
         norm2 = [sb.tile([P, V], F32, name=f"norm2{h}") for h in range(BLOCKS)]
-        num = sb.tile([P, BLOCKS, V], F32, name="num")
-        inv = [sb.tile([P, V], F32, name=f"inv{h}") for h in range(BLOCKS)]
+        num = [sb.tile([P, V], F32, name=f"num{h}") for h in range(BLOCKS)]
+        inv = [sb.tile([P, V], F32, name="inv0", tag="both111"), sb.tile([P, V], F32, name="inv1")]
         res = [sb.tile([P, V], F32, name=f"res{h}") for h in range(BLOCKS)]
-        nc.scalar.activation(squares[0][:], acc[0][:], ACT.Square)
-        nc.vector.tensor_tensor(scaled[:, :, 1, :], acc[1][:], spread, ALU.mult)
-        nc.scalar.activation(squares[1][:], acc[1][:], ACT.Square)
-        nc.vector.tensor_tensor(scaled[:, :, 0, :], acc[0][:], spread, ALU.mult)
+        nc.scalar.activation(squares[0][:], acc0[:], ACT.Square)
+        for i in range(2):
+            nc.scalar.activation(squares[1][:, i], acc[1, i], ACT.Square)
+        nc.vector.tensor_tensor(norm2[0][:], squares[0][:, 0], squares[0][:, 1], ALU.add)
+        nc.vector.tensor_tensor(scaled[0][:], acc0[:], spread[:], ALU.mult)
+        nc.vector.tensor_tensor(scaled[1][:, 0], acc[1, 0], spread[:, 0], ALU.mult)
+        nc.vector.tensor_tensor(num[0][:], scaled[0][:, 0], scaled[0][:, 1], ALU.add)
+        nc.vector.tensor_tensor(norm2[1][:], squares[1][:, 0], squares[1][:, 1], ALU.add)
+        nc.vector.tensor_tensor(scaled[1][:, 1], acc[1, 1], spread[:, 1], ALU.mult)
         for h in range(BLOCKS):
-            nc.vector.tensor_tensor(norm2[h][:], squares[h][:, 0, :], squares[h][:, 1, :], ALU.add)
             nc.scalar.activation(inv[h][:], norm2[h][:], ACT.Abs_reciprocal_sqrt, bias=0.1)
-        nc.vector.tensor_tensor(num[:], scaled[:, 0], scaled[:, 1], ALU.add)
-        for h in range(BLOCKS):
-            nc.vector.tensor_tensor(res[h][:], num[:, h, :], inv[h][:], ALU.mult)
-            nc.sync.dma_start(out=out[h * P : (h + 1) * P, :], in_=res[h][:])
+        nc.vector.tensor_tensor(res[0][:], num[0][:], inv[0][:], ALU.mult)
+        nc.sync.dma_start(out=out[0:P, :], in_=res[0][:])
+        nc.vector.tensor_tensor(num[1][:], scaled[1][:, 0], scaled[1][:, 1], ALU.add)
+        nc.vector.tensor_tensor(res[1][:], num[1][:], inv[1][:], ALU.mult)
+        nc.sync.dma_start(out=out[P : 2 * P, :], in_=res[1][:])

@@ -32,182 +32,163 @@ def tile_picked_yarap_rhs_p_kernel(
         sb = ctx.enter_context(tc.tile_pool(name="sb", bufs=1))
         ps = ctx.enter_context(tc.psum_pool(name="ps", bufs=1))
 
+        def tile(shape, dtype, name, tag=None):
+            return sb.tile(shape, dtype, name=name, tag=tag or name, align_bytes=64)
+
+        pieces = [(o, h, c) for h in range(BLOCKS) for o in range(PASSES) for c in range(2)]
         offsets = sb.tile([P, S // 16], U16, name="offsets")
-        x_table = [sb.tile([P, T], U32, name=f"x_table{o}", align_bytes=64) for o in range(PASSES)]
-        s_table = sb.tile([P, T], U8, name="s_table")
-        raw0 = [sb.tile([P, PACK, N], F32, name=f"raw0_{c}", align_bytes=64) for c in range(2)]
-        raw1 = {(h, c): sb.tile([P, PACK, P], F32, name=f"raw1_{h}{c}", align_bytes=64) for h in range(BLOCKS) for c in range(2)}
-        w_codes = {(o, h): sb.tile([P, 2 * P], U32, name=f"w_codes{o}{h}", align_bytes=64) for o in range(PASSES) for h in range(BLOCKS)}
-        w_scales = {(o, h): sb.tile([P, 2 * P], U8, name=f"w_scales{o}{h}", align_bytes=64) for o in range(PASSES) for h in range(BLOCKS)}
-        w_bf = {}
-        x_codes = [sb.tile([P, S], U32, name=f"x_codes{o}", align_bytes=64) for o in range(PASSES)]
-        x_picked = []
-        s_picked = sb.tile([P, S], U8, name="s_picked", align_bytes=64)
-        s_dealt = sb.tile([P, S], U8, name="s_dealt", align_bytes=64)
-        ident = sb.tile([P, P], F32, name="ident")
-        cot_t = sb.tile([P, D], F32, name="cot_t")
-        rest = sb.tile([P, 2, 8], F32, name="rest")
+        x_table = [tile([P, T], U32, f"x_table{o}") for o in range(PASSES)]
+        s_table = tile([P, T], U8, "s_table")
+        w_raw = {(o, h, c): tile([P, PACK, P], F32, f"w_raw{o}{h}{c}") for o, h, c in pieces}
+        cot_t = tile([P, D], F32, "cot_t")
+        rest = tile([P, 2, 8], F32, "rest")
+        ident = tile([P, P], F32, "ident")
 
         def load_x(o):
             nc.sync.dma_start(out=x_table[o][:].bitcast(I32), in_=x_words[o].rearrange("p n t -> p (n t)").bitcast(I32))
 
-        def load_w(dst, c, o, cols):
-            rows = weights[c][o * P * PACK : (o + 1) * P * PACK, cols]
-            nc.sync.dma_start(out=dst[:], in_=rows.rearrange("(p t) m -> p t m", t=PACK))
-
-        def load_small():
-            for dst, row in ((cot_t[:], cot), (rest[:, 0, 0:D], rx), (rest[:, 1, 0:D], ry)):
-                nc.sync.dma_start(out=dst, in_=row[0].rearrange("(v d) -> v d", d=D))
+        def load_w(o, h, c):
+            rows = weights[c][o * P * PACK : (o + 1) * P * PACK, h * P : (h + 1) * P]
+            nc.sync.dma_start(out=w_raw[o, h, c][:], in_=rows.rearrange("(p t) m -> p t m", t=PACK))
 
         nc.vector.memset(s_table[:].bitcast(I32), 0)
         nc.sync.dma_start(offsets[:], offs)
+        for dst, row in ((cot_t[:], cot), (rest[:, 0, 0:D], rx), (rest[:, 1, 0:D], ry)):
+            nc.sync.dma_start(out=dst, in_=row[0].rearrange("(v d) -> v d", d=D))
         load_x(0)
         for q in range(4):
             nc.sync.dma_start(
                 out=s_table[32 * q : 32 * q + 4 * PASSES, :].bitcast(I32),
                 in_=x_scales[:, 4 * q : 4 * q + 4, :].bitcast(I32),
             )
-        for c in range(2):
-            load_w(raw0[c], c, 0, slice(0, N))
-        load_small()
+        for piece in pieces[:2]:
+            load_w(*piece)
         load_x(1)
-        for h in range(BLOCKS):
-            for c in range(2):
-                load_w(raw1[h, c], c, 1, slice(h * P, (h + 1) * P))
+        for piece in pieces[2:]:
+            load_w(*piece)
+        warm = tile([P, 2], F32, "warm")
+        nc.gpsimd.memset(warm[:, 0:1], 1.0)
+        nc.scalar.activation(warm[:, 1:2], warm[:, 0:1], ACT.Abs_reciprocal_sqrt, bias=0.1)
+
         make_identity(nc, ident[:])
 
-        warm = sb.tile([P, 1], F32, name="warm")
-        nc.scalar.activation(warm[:], ident[:, 0:1], ACT.Abs_reciprocal_sqrt, bias=0.1)
-
-        acc0 = ps.tile([P, 2, V], F32, name="acc0")
-        acc1 = [ps.tile([P, V], F32, name=f"acc1{i}") for i in range(2)]
-        acc = {(0, 0): acc0[:, 0], (0, 1): acc0[:, 1], (1, 0): acc1[0][:], (1, 1): acc1[1][:]}
-        yz_bank = {(h, e): ps.tile([P, 2, 2, P], F32, name=f"yz_bank{h}{e}") for h in range(BLOCKS) for e in range(2)}
+        factors = tile([P, 4, D], F32, "factors", "warm")
+        sums = tile([P, 2], F32, "sums")
+        a, b, nb = factors[:, 0, :], factors[:, 1, :], factors[:, 2, :]
+        for d in range(D):
+            nc.scalar.activation(factors[:, 0:2, d], rest[:, :, d], ACT.Copy, scale=cot_t[:, d : d + 1])
+        nc.scalar.activation(factors[:, 3, :], a, ACT.Copy, accum_out=sums[:, 0:1])
+        nc.scalar.activation(nb, b, ACT.Copy, scale=-1.0, accum_out=sums[:, 1:2])
         spread_ps = ps.tile([P, 2, V], F32, name="spread_ps")
-        yz_of = {(h, d): yz_bank[h, d % 2][:, d // 2] for h in range(BLOCKS) for d in range(D)}
-        alone = ((1, 1), (1, 3))
+        for i in range(2):
+            nc.tensor.transpose(spread_ps[:, i, :], sums[:, i : i + 1].to_broadcast([P, P]), ident[:])
+        spread = tile([P, 2, V], F32, "spread")
+        nc.scalar.copy(spread[:], spread_ps[:])
 
-        def gather_words(o):
+        yz = {}
+        for h in range(BLOCKS):
+            even = ps.tile([P, 2, 2, P], F32, name=f"even{h}")
+            yz[h, 0], yz[h, 2] = even[:, 0], even[:, 1]
+            for d in (1, 3):
+                yz[h, d] = ps.tile([P, 2, P], F32, name=f"odd{h}{d}")[:]
+
+        x_picked, x_codes, w_codes, w_scales = {}, {}, {}, {}
+
+        def gather_words(o, tag=None):
+            x_picked[o] = tile([P, S], U32, f"x_picked{o}", tag)
             nc.vector.tensor_copy(x_picked[o][:], x_table[o][:].indirect(offsets[:]))
 
-        def deal(dst, src, run):
+        def deal(src, dtype, name, run):
+            dst = tile([P, S], dtype, name)
             nc.vector.tensor_copy(
                 dst[:].rearrange("p (d g i) -> p g d i", d=D, i=run),
                 src[:].rearrange("p (g i d) -> p g d i", d=D, i=run),
             )
+            return dst
 
-        def cast(o, h, c, copy):
-            src = raw0[c][:, :, h * P : (h + 1) * P] if o == 0 else raw1[h, c][:]
-            copy(
-                w_bf[o, h][:, c].rearrange("p (g i) t -> p g t i", i=4),
-                src.rearrange("p t (g i) -> p g t i", i=4),
-            )
+        def cast(dst, piece, copy):
+            copy(dst.rearrange("p (g i) t -> p g t i", i=4), w_raw[piece][:].rearrange("p t (g i) -> p g t i", i=4))
 
-        def quantise(o, h):
-            nc.vector.quantize_mx(
-                out=w_codes[o, h][:].bitcast(FP8X4),
-                scales=w_scales[o, h][:],
-                in_=w_bf[o, h][:].rearrange("p c m t -> p (c m t)"),
-            )
+        def mx_tiles(o, h, codes_tag=None, scales_tag=None):
+            w_codes[o, h] = tile([P, 2 * P], U32, f"w_codes{o}{h}", codes_tag)
+            w_scales[o, h] = tile([P, 2 * P], U8, f"w_scales{o}{h}", scales_tag)
+
+        def quantise(o, h, cols, src):
+            nc.vector.quantize_mx(out=w_codes[o, h][:, cols].bitcast(FP8X4), scales=w_scales[o, h][:, cols], in_=src)
 
         def products(o, h):
-            for e in range(2):
-                for f in range(2):
-                    d = 2 * f + e
-                    cols = slice(d * V, (d + 1) * V)
-                    nc.tensor.matmul_mx(
-                        out=yz_of[h, d].rearrange("p c m -> p (c m)"),
-                        lhsT=x_codes[o][:, cols].bitcast(FP8X4),
-                        lhsT_scale=s_dealt[4 * o :, cols],
-                        rhs=w_codes[o, h][:].bitcast(FP8X4),
-                        rhs_scale=w_scales[o, h][:],
-                        start=(o == 0 and (f == 0 or (h, d) in alone)),
-                        stop=(o == PASSES - 1 and (f == 1 or (h, d) in alone)),
-                    )
+            for d in (0, 2, 3, 1):
+                cols = slice(d * V, (d + 1) * V)
+                nc.tensor.matmul_mx(
+                    out=yz[h, d].rearrange("p c m -> p (c m)"),
+                    lhsT=x_codes[o][:, cols].bitcast(FP8X4),
+                    lhsT_scale=s_dealt[4 * o :, cols],
+                    rhs=w_codes[o, h][:].bitcast(FP8X4),
+                    rhs_scale=w_scales[o, h][:],
+                    start=(o == 0 and d != 2),
+                    stop=(o == PASSES - 1 and d != 0),
+                )
 
-        def bf_tile(o, h, tag=""):
-            w_bf[o, h] = sb.tile([P, 2, P, PACK], BF16, name=f"w_bf{o}{h}", tag=tag or f"w_bf{o}{h}", align_bytes=64)
+        def block0_pass(o, codes_tag=None):
+            both = tile([P, 2, P, PACK], BF16, f"w_bf{o}0")
+            for c in range(2):
+                cast(both[:, c], (o, 0, c), nc.scalar.copy)
+            mx_tiles(o, 0, codes_tag)
+            quantise(o, 0, slice(0, 2 * P), both[:].rearrange("p c m t -> p (c m t)"))
+            products(o, 0)
 
-        x_picked.append(sb.tile([P, S], U32, name="x_picked0", align_bytes=64))
+        def block1_pass(o, codes_tag=None, scales_tag=None):
+            halves = [tile([P, P, PACK], BF16, f"w_bf{o}10"), tile([P, P, PACK], BF16, f"w_bf{o}11", "w_bf10")]
+            mx_tiles(o, 1, codes_tag, scales_tag)
+            for c, copy in enumerate((nc.scalar.copy, nc.vector.tensor_copy)):
+                cast(halves[c][:], (o, 1, c), copy)
+                quantise(o, 1, slice(c * P, (c + 1) * P), halves[c][:].rearrange("p m t -> p (m t)"))
+            products(o, 1)
+
         gather_words(0)
+        s_picked = tile([P, S], U8, "s_picked")
         nc.vector.tensor_copy(s_picked[:], s_table[:].indirect(offsets[:]))
-        deal(x_codes[0], x_picked[0], 4)
-        deal(s_dealt, s_picked, 16)
-        for h in range(BLOCKS):
-            bf_tile(0, h)
-        for c in range(2):
-            for h in range(BLOCKS):
-                cast(0, h, c, nc.scalar.copy)
-        for h in range(BLOCKS):
-            quantise(0, h)
-        products(0, 0)
-        coef3 = sb.tile([P, 4, D], F32, name="coef3", tag="raw0_1", align_bytes=64)
-        sums = sb.tile([P, 2], F32, name="sums")
-        a, b, nb = coef3[:, 0, :], coef3[:, 1, :], coef3[:, 2, :]
-        for d in range(D):
-            nc.scalar.activation(coef3[:, 0:2, d], rest[:, :, d], ACT.Copy, scale=cot_t[:, d : d + 1])
-        nc.scalar.activation(coef3[:, 3, :], a, ACT.Copy, accum_out=sums[:, 0:1])
-        nc.scalar.activation(nb, b, ACT.Copy, scale=-1.0, accum_out=sums[:, 1:2])
-        for i in range(2):
-            nc.tensor.transpose(spread_ps[:, i, :], sums[:, i : i + 1].to_broadcast([P, P]), ident[:])
-        spread = sb.tile([P, 2, V], F32, name="spread")
-        nc.scalar.copy(spread[:], spread_ps[:])
-        last_bank = ps.tile([P, 2, P], F32, name="last_bank", tag="spread_ps")
-        yz_of[1, 3] = last_bank[:]
-        products(0, 1)
-        x_picked.append(sb.tile([P, S], U32, name="x_picked1", tag="w_bf01", align_bytes=64))
-        gather_words(1)
+        x_codes[0] = deal(x_picked[0], U32, "x_codes0", 4)
+        s_dealt = deal(s_picked, U8, "s_dealt", 16)
+        block0_pass(0)
+        gather_words(1, "w_bf00")
+        x_codes[1] = deal(x_picked[1], U32, "x_codes1", 4)
+        block0_pass(1, codes_tag="x_table1")
+        block1_pass(0, codes_tag="w_bf00")
+        block1_pass(1, scales_tag="w_raw011")
 
-        bf_tile(1, 0, "x_table1")
-        cast(1, 0, 0, nc.scalar.copy)
-        cast(1, 0, 1, nc.vector.tensor_copy)
-        deal(x_codes[1], x_picked[1], 4)
-        quantise(1, 0)
-        products(1, 0)
-        bf_tile(1, 1, "raw1_00")
-        cast(1, 1, 0, nc.scalar.copy)
-        cast(1, 1, 1, nc.vector.tensor_copy)
-        for c in range(2):
-            nc.vector.quantize_mx(
-                out=w_codes[1, 1][:, c * P : (c + 1) * P].bitcast(FP8X4),
-                scales=w_scales[1, 1][:, c * P : (c + 1) * P],
-                in_=w_bf[1, 1][:, c].rearrange("p m t -> p (m t)"),
-            )
-        products(1, 1)
-
-        def add_terms(h, terms):
-            for n, (i, term) in enumerate(terms):
-                mine = [m for m, (j, other) in enumerate(terms) if h == 0 or j == i]
-                nc.tensor.matmul(acc[h, i], term, ident[:], is_transpose=True, start=(n == mine[0]), stop=(n == mine[-1]))
-
+        acc0 = ps.tile([P, 2, V], F32, name="acc0")
+        acc = {(0, 0): acc0[:, 0], (0, 1): acc0[:, 1]}
         for h in range(BLOCKS):
-            terms = []
-            for f in range(2):
-                d, e = 2 * f, 2 * f + 1
-                own = [sb.tile([P, 2, P], F32, name=f"own{h}{f}{n}") for n in range(2)]
-                both = [sb.tile([P, 2, P], F32, name=f"both{h}{f}{n}") for n in range(2)]
-                yz = yz_of[h, e]
-                if (h, e) == (1, 3):
-                    nc.scalar.activation(own[1][:], yz_of[h, d], ACT.Copy, scale=b[:, d : d + 1])
-                    nc.scalar.activation(both[0][:], yz, ACT.Copy, scale=a[:, e : e + 1])
-                    nc.scalar.activation(own[0][:], yz_of[h, d], ACT.Copy, scale=a[:, d : d + 1])
-                    terms.extend([(0, both[0][:, 0]), (1, both[0][:, 1]), (0, own[0][:, 0]), (1, own[0][:, 1])])
+            names = ("a0", "b0", "b2", "a3", "a2", "a1", "b1", "b3")
+            t = {n: tile([P, 2, P], F32, f"{n}_{h}", "w_bf10" if (n, h) == ("a1", 0) else None) for n in names}
+            for n in names[:5]:
+                d = int(n[1])
+                if (n, h) == ("a3", 1):
+                    nc.vector.tensor_scalar(t[n][:], yz[h, d], a[:, d : d + 1], None, ALU.mult)
                 else:
-                    for n, coef in enumerate((a, b)):
-                        nc.scalar.activation(own[n][:], yz_of[h, d], ACT.Copy, scale=coef[:, d : d + 1])
-                    nc.vector.scalar_tensor_tensor(both[0][:], yz, a[:, e : e + 1], own[0][:], ALU.mult, ALU.add)
-                    terms.extend([(0, both[0][:, 0]), (1, both[0][:, 1])])
-                nc.vector.scalar_tensor_tensor(both[1][:, 0], yz[:, 1], b[:, e : e + 1], own[1][:, 1], ALU.mult, ALU.add)
-                nc.vector.scalar_tensor_tensor(both[1][:, 1], yz[:, 0], nb[:, e : e + 1], own[1][:, 0], ALU.mult, ALU.subtract)
-                terms.extend([(0, both[1][:, 0]), (1, both[1][:, 1])])
-            add_terms(h, terms)
+                    nc.scalar.activation(t[n][:], yz[h, d], ACT.Copy, scale=(a if n[0] == "a" else b)[:, d : d + 1])
+            nc.vector.scalar_tensor_tensor(t["a1"][:], yz[h, 1], a[:, 1:2], t["a0"][:], ALU.mult, ALU.add)
+            for d in (1, 3):
+                new, old = t[f"b{d}"], t[f"b{d - 1}"]
+                nc.vector.scalar_tensor_tensor(new[:, 0], yz[h, d][:, 1], b[:, d : d + 1], old[:, 1], ALU.mult, ALU.add)
+                nc.vector.scalar_tensor_tensor(new[:, 1], yz[h, d][:, 0], nb[:, d : d + 1], old[:, 0], ALU.mult, ALU.subtract)
+            if h == 1:
+                acc[1, 0] = ps.tile([P, V], F32, name="acc10", tag="even0")[:]
+                acc[1, 1] = ps.tile([P, V], F32, name="acc11", tag="spread_ps")[:]
+            order = (("a1", "a3", "a2", "b1", "b3"), ("a3", "a1", "b1", "a2", "b3"))[h]
+            for n in order:
+                for i in range(2):
+                    first = n == order[0] and (h == 1 or i == 0)
+                    last = n == order[-1] and (h == 1 or i == 1)
+                    nc.tensor.matmul(acc[h, i], t[n][:, i], ident[:], is_transpose=True, start=first, stop=last)
 
-        squares = [sb.tile([P, 2, V], F32, name=f"squares{h}") for h in range(BLOCKS)]
-        scaled = [sb.tile([P, 2, V], F32, name=f"scaled{h}") for h in range(BLOCKS)]
-        norm2 = [sb.tile([P, V], F32, name=f"norm2{h}") for h in range(BLOCKS)]
-        num = [sb.tile([P, V], F32, name=f"num{h}") for h in range(BLOCKS)]
-        inv = [sb.tile([P, V], F32, name="inv0", tag="both111"), sb.tile([P, V], F32, name="inv1")]
-        res = [sb.tile([P, V], F32, name=f"res{h}") for h in range(BLOCKS)]
+        squares = [tile([P, 2, V], F32, f"squares{h}") for h in range(BLOCKS)]
+        scaled = [tile([P, 2, V], F32, f"scaled{h}") for h in range(BLOCKS)]
+        norm2 = [tile([P, V], F32, f"norm2{h}") for h in range(BLOCKS)]
+        num = [tile([P, V], F32, f"num{h}") for h in range(BLOCKS)]
+        inv = [tile([P, V], F32, "inv0", "b3_1"), tile([P, V], F32, "inv1")]
+        res = [tile([P, V], F32, f"res{h}") for h in range(BLOCKS)]
         nc.scalar.activation(squares[0][:], acc0[:], ACT.Square)
         for i in range(2):
             nc.scalar.activation(squares[1][:, i], acc[1, i], ACT.Square)
@@ -219,8 +200,7 @@ def tile_picked_yarap_rhs_p_kernel(
         nc.vector.tensor_tensor(scaled[1][:, 1], acc[1, 1], spread[:, 1], ALU.mult)
         for h in range(BLOCKS):
             nc.scalar.activation(inv[h][:], norm2[h][:], ACT.Abs_reciprocal_sqrt, bias=0.1)
-        nc.vector.tensor_tensor(res[0][:], num[0][:], inv[0][:], ALU.mult)
-        nc.sync.dma_start(out=out[0:P, :], in_=res[0][:])
         nc.vector.tensor_tensor(num[1][:], scaled[1][:, 0], scaled[1][:, 1], ALU.add)
-        nc.vector.tensor_tensor(res[1][:], num[1][:], inv[1][:], ALU.mult)
-        nc.sync.dma_start(out=out[P : 2 * P, :], in_=res[1][:])
+        for h in range(BLOCKS):
+            nc.vector.tensor_tensor(res[h][:], num[h][:], inv[h][:], ALU.mult)
+            nc.sync.dma_start(out=out[h * P : (h + 1) * P, :], in_=res[h][:])

@@ -35,11 +35,13 @@ def tile_picked_yarap_rhs_p_kernel(
         def tile(shape, dtype, name, tag=None):
             return sb.tile(shape, dtype, name=name, tag=tag or name, align_bytes=64)
 
-        pieces = [(o, h, c) for h in range(BLOCKS) for o in range(PASSES) for c in range(2)]
         offsets = sb.tile([P, S // 16], U16, name="offsets")
         x_table = [tile([P, T], U32, f"x_table{o}") for o in range(PASSES)]
         s_table = tile([P, T], U8, "s_table")
-        w_raw = {(o, h, c): tile([P, PACK, P], F32, f"w_raw{o}{h}{c}") for o, h, c in pieces}
+        first_raw = [tile([P, PACK, N], F32, f"w_raw0{c}") for c in range(2)]
+        last_raw = {(h, c): tile([P, PACK, P], F32, f"w_raw1{h}{c}") for h in range(BLOCKS) for c in range(2)}
+        w_raw = {(0, h, c): first_raw[c][:, :, h * P : (h + 1) * P] for h in range(BLOCKS) for c in range(2)}
+        w_raw.update({(1, h, c): last_raw[h, c][:] for h, c in last_raw})
         cot_t = tile([P, D], F32, "cot_t")
         rest = tile([P, 2, 8], F32, "rest")
         ident = tile([P, P], F32, "ident")
@@ -47,43 +49,30 @@ def tile_picked_yarap_rhs_p_kernel(
         def load_x(o):
             nc.sync.dma_start(out=x_table[o][:].bitcast(I32), in_=x_words[o].rearrange("p n t -> p (n t)").bitcast(I32))
 
-        def load_w(o, h, c):
-            rows = weights[c][o * P * PACK : (o + 1) * P * PACK, h * P : (h + 1) * P]
-            nc.sync.dma_start(out=w_raw[o, h, c][:], in_=rows.rearrange("(p t) m -> p t m", t=PACK))
+        def load_w(dst, o, c, cols):
+            rows = weights[c][o * P * PACK : (o + 1) * P * PACK, cols]
+            nc.sync.dma_start(out=dst[:], in_=rows.rearrange("(p t) m -> p t m", t=PACK))
 
         nc.vector.memset(s_table[:].bitcast(I32), 0)
-        nc.sync.dma_start(offsets[:], offs)
-        for dst, row in ((cot_t[:], cot), (rest[:, 0, 0:D], rx), (rest[:, 1, 0:D], ry)):
-            nc.sync.dma_start(out=dst, in_=row[0].rearrange("(v d) -> v d", d=D))
         load_x(0)
+        nc.sync.dma_start(offsets[:], offs)
         for q in range(4):
             nc.sync.dma_start(
                 out=s_table[32 * q : 32 * q + 4 * PASSES, :].bitcast(I32),
                 in_=x_scales[:, 4 * q : 4 * q + 4, :].bitcast(I32),
             )
-        for piece in pieces[:2]:
-            load_w(*piece)
+        for c in range(2):
+            load_w(first_raw[c], 0, c, slice(0, N))
+        for dst, row in ((cot_t[:], cot), (rest[:, 0, 0:D], rx), (rest[:, 1, 0:D], ry)):
+            nc.sync.dma_start(out=dst, in_=row[0].rearrange("(v d) -> v d", d=D))
         load_x(1)
-        for piece in pieces[2:]:
-            load_w(*piece)
+        for h, c in last_raw:
+            load_w(last_raw[h, c], 1, c, slice(h * P, (h + 1) * P))
         warm = tile([P, 2], F32, "warm")
         nc.gpsimd.memset(warm[:, 0:1], 1.0)
         nc.scalar.activation(warm[:, 1:2], warm[:, 0:1], ACT.Abs_reciprocal_sqrt, bias=0.1)
 
         make_identity(nc, ident[:])
-
-        factors = tile([P, 4, D], F32, "factors", "warm")
-        sums = tile([P, 2], F32, "sums")
-        a, b, nb = factors[:, 0, :], factors[:, 1, :], factors[:, 2, :]
-        for d in range(D):
-            nc.scalar.activation(factors[:, 0:2, d], rest[:, :, d], ACT.Copy, scale=cot_t[:, d : d + 1])
-        nc.scalar.activation(factors[:, 3, :], a, ACT.Copy, accum_out=sums[:, 0:1])
-        nc.scalar.activation(nb, b, ACT.Copy, scale=-1.0, accum_out=sums[:, 1:2])
-        spread_ps = ps.tile([P, 2, V], F32, name="spread_ps")
-        for i in range(2):
-            nc.tensor.transpose(spread_ps[:, i, :], sums[:, i : i + 1].to_broadcast([P, P]), ident[:])
-        spread = tile([P, 2, V], F32, "spread")
-        nc.scalar.copy(spread[:], spread_ps[:])
 
         yz = {}
         for h in range(BLOCKS):
@@ -107,7 +96,7 @@ def tile_picked_yarap_rhs_p_kernel(
             return dst
 
         def cast(dst, piece, copy):
-            copy(dst.rearrange("p (g i) t -> p g t i", i=4), w_raw[piece][:].rearrange("p t (g i) -> p g t i", i=4))
+            copy(dst.rearrange("p (g i) t -> p g t i", i=4), w_raw[piece].rearrange("p t (g i) -> p g t i", i=4))
 
         def mx_tiles(o, h, codes_tag=None, scales_tag=None):
             w_codes[o, h] = tile([P, 2 * P], U32, f"w_codes{o}{h}", codes_tag)
@@ -129,39 +118,66 @@ def tile_picked_yarap_rhs_p_kernel(
                     stop=(o == PASSES - 1 and d != 0),
                 )
 
-        def block0_pass(o, codes_tag=None):
-            both = tile([P, 2, P, PACK], BF16, f"w_bf{o}0")
-            for c in range(2):
-                cast(both[:, c], (o, 0, c), nc.scalar.copy)
-            mx_tiles(o, 0, codes_tag)
-            quantise(o, 0, slice(0, 2 * P), both[:].rearrange("p c m t -> p (c m t)"))
-            products(o, 0)
-
-        def block1_pass(o, codes_tag=None, scales_tag=None):
-            halves = [tile([P, P, PACK], BF16, f"w_bf{o}10"), tile([P, P, PACK], BF16, f"w_bf{o}11", "w_bf10")]
-            mx_tiles(o, 1, codes_tag, scales_tag)
-            for c, copy in enumerate((nc.scalar.copy, nc.vector.tensor_copy)):
-                cast(halves[c][:], (o, 1, c), copy)
-                quantise(o, 1, slice(c * P, (c + 1) * P), halves[c][:].rearrange("p m t -> p (m t)"))
-            products(o, 1)
-
         gather_words(0)
         s_picked = tile([P, S], U8, "s_picked")
         nc.vector.tensor_copy(s_picked[:], s_table[:].indirect(offsets[:]))
         x_codes[0] = deal(x_picked[0], U32, "x_codes0", 4)
         s_dealt = deal(s_picked, U8, "s_dealt", 16)
-        block0_pass(0)
-        gather_words(1, "w_bf00")
-        x_codes[1] = deal(x_picked[1], U32, "x_codes1", 4)
-        block0_pass(1, codes_tag="x_table1")
-        block1_pass(0, codes_tag="w_bf00")
-        block1_pass(1, scales_tag="w_raw011")
+        first_bf = [tile([P, 2, P, PACK], BF16, f"w_bf0{h}") for h in range(BLOCKS)]
+        for c in range(2):
+            for h in range(BLOCKS):
+                cast(first_bf[h][:, c], (0, h, c), nc.scalar.copy)
+        for h in range(BLOCKS):
+            mx_tiles(0, h)
+            quantise(0, h, slice(0, 2 * P), first_bf[h][:].rearrange("p c m t -> p (c m t)"))
+            products(0, h)
 
-        acc0 = ps.tile([P, 2, V], F32, name="acc0")
+        factors = tile([P, 4, D], F32, "factors", "w_raw01")
+        sums = tile([P, 2], F32, "sums")
+        a, b, nb = factors[:, 0, :], factors[:, 1, :], factors[:, 2, :]
+        for d in range(D):
+            nc.scalar.activation(factors[:, 0:2, d], rest[:, :, d], ACT.Copy, scale=cot_t[:, d : d + 1])
+        nc.scalar.activation(factors[:, 3, :], a, ACT.Copy, accum_out=sums[:, 0:1])
+        nc.scalar.activation(nb, b, ACT.Copy, scale=-1.0, accum_out=sums[:, 1:2])
+        spread_ps = ps.tile([P, 2, V], F32, name="spread_ps")
+        for i in range(2):
+            nc.tensor.transpose(spread_ps[:, i, :], sums[:, i : i + 1].to_broadcast([P, P]), ident[:])
+        spread = tile([P, 2, V], F32, "spread")
+        nc.scalar.copy(spread[:], spread_ps[:])
+
+        gather_words(1, "w_bf01")
+        warm_ps = ps.tile([P, 2 * P], F32, name="warm_ps")
+        for d in range(D):
+            cols = slice(d * V, (d + 1) * V)
+            nc.tensor.matmul_mx(
+                out=warm_ps[:],
+                lhsT=x_picked[1][:, cols].bitcast(FP8X4),
+                lhsT_scale=s_picked[4:, cols],
+                rhs=w_codes[0, 1][:].bitcast(FP8X4),
+                rhs_scale=w_scales[0, 1][:],
+                start=True,
+                stop=True,
+            )
+        x_codes[1] = deal(x_picked[1], U32, "x_codes1", 4)
+        block0_bf = tile([P, 2, P, PACK], BF16, "w_bf10", "w_bf00")
+        for c in range(2):
+            cast(block0_bf[:, c], (1, 0, c), nc.scalar.copy)
+        mx_tiles(1, 0, codes_tag="x_table1")
+        quantise(1, 0, slice(0, 2 * P), block0_bf[:].rearrange("p c m t -> p (c m t)"))
+        products(1, 0)
+        halves = [tile([P, P, PACK], BF16, "w_bf110"), tile([P, P, PACK], BF16, "w_bf111", "w_bf00")]
+        mx_tiles(1, 1, scales_tag="w_bf01")
+        for c, copy in ((1, nc.vector.tensor_copy), (0, nc.scalar.copy)):
+            cast(halves[c][:], (1, 1, c), copy)
+        for c in range(2):
+            quantise(1, 1, slice(c * P, (c + 1) * P), halves[c][:].rearrange("p m t -> p (m t)"))
+        products(1, 1)
+
+        acc0 = ps.tile([P, 2, V], F32, name="acc0", tag="warm_ps")
         acc = {(0, 0): acc0[:, 0], (0, 1): acc0[:, 1]}
         for h in range(BLOCKS):
             names = ("a0", "b0", "b2", "a3", "a2", "a1", "b1", "b3")
-            t = {n: tile([P, 2, P], F32, f"{n}_{h}", "w_bf10" if (n, h) == ("a1", 0) else None) for n in names}
+            t = {n: tile([P, 2, P], F32, f"{n}_{h}", "w_bf00" if (n, h) == ("a1", 0) else None) for n in names}
             for n in names[:5]:
                 d = int(n[1])
                 if (n, h) == ("a3", 1):

@@ -20,7 +20,10 @@ P = 128
 PACK = 4
 PASSES = K // (P * PACK)
 V = S // D
-BLOCKS = N // P
+HALVES = N // P
+QUADRANTS = 4
+LINE = 16
+EPSILON = 0.1
 
 
 def tile_picked_yarap_rhs_p_kernel(
@@ -32,18 +35,18 @@ def tile_picked_yarap_rhs_p_kernel(
         sb = ctx.enter_context(tc.tile_pool(name="sb", bufs=1))
         ps = ctx.enter_context(tc.psum_pool(name="ps", bufs=1))
 
-        def tile(shape, dtype, name, tag=None):
-            return sb.tile(shape, dtype, name=name, tag=tag or name, align_bytes=64)
+        def tile(shape, dtype, name, after=None):
+            return sb.tile(shape, dtype, name=name, tag=after or name, align_bytes=64)
 
         offsets = sb.tile([P, S // 16], U16, name="offsets")
         x_table = [tile([P, T], U32, f"x_table{o}") for o in range(PASSES)]
         s_table = tile([P, T], U8, "s_table")
         first_raw = [tile([P, PACK, N], F32, f"w_raw0{c}") for c in range(2)]
-        last_raw = {(h, c): tile([P, PACK, P], F32, f"w_raw1{h}{c}") for h in range(BLOCKS) for c in range(2)}
-        w_raw = {(0, h, c): first_raw[c][:, :, h * P : (h + 1) * P] for h in range(BLOCKS) for c in range(2)}
+        last_raw = {(h, c): tile([P, PACK, P], F32, f"w_raw1{h}{c}") for h in range(HALVES) for c in range(2)}
+        w_raw = {(0, h, c): first_raw[c][:, :, h * P : (h + 1) * P] for h in range(HALVES) for c in range(2)}
         w_raw.update({(1, h, c): last_raw[h, c][:] for h, c in last_raw})
         cot_t = tile([P, D], F32, "cot_t")
-        rest = tile([P, 2, 8], F32, "rest")
+        rest = tile([P, 2, 2 * D], F32, "rest")
         ident = tile([P, P], F32, "ident")
 
         def load_x(o):
@@ -56,26 +59,27 @@ def tile_picked_yarap_rhs_p_kernel(
         nc.vector.memset(s_table[:].bitcast(I32), 0)
         load_x(0)
         nc.sync.dma_start(offsets[:], offs)
-        for q in range(4):
+        for q in range(QUADRANTS):
             nc.sync.dma_start(
-                out=s_table[32 * q : 32 * q + 4 * PASSES, :].bitcast(I32),
-                in_=x_scales[:, 4 * q : 4 * q + 4, :].bitcast(I32),
+                out=s_table[32 * q : 32 * q + PACK * PASSES, :].bitcast(I32),
+                in_=x_scales[:, PACK * q : PACK * (q + 1), :].bitcast(I32),
             )
         for c in range(2):
             load_w(first_raw[c], 0, c, slice(0, N))
-        for dst, row in ((cot_t[:], cot), (rest[:, 0, 0:D], rx), (rest[:, 1, 0:D], ry)):
-            nc.sync.dma_start(out=dst, in_=row[0].rearrange("(v d) -> v d", d=D))
+        for dst, rows in ((cot_t[:], cot), (rest[:, 0, 0:D], rx), (rest[:, 1, 0:D], ry)):
+            nc.sync.dma_start(out=dst, in_=rows[0].rearrange("(v d) -> v d", d=D))
         load_x(1)
         for h, c in last_raw:
             load_w(last_raw[h, c], 1, c, slice(h * P, (h + 1) * P))
+
         warm = tile([P, 2], F32, "warm")
         nc.gpsimd.memset(warm[:, 0:1], 1.0)
-        nc.scalar.activation(warm[:, 1:2], warm[:, 0:1], ACT.Abs_reciprocal_sqrt, bias=0.1)
+        nc.scalar.activation(warm[:, 1:2], warm[:, 0:1], ACT.Abs_reciprocal_sqrt, bias=EPSILON)
 
         make_identity(nc, ident[:])
 
         yz = {}
-        for h in range(BLOCKS):
+        for h in range(HALVES):
             even = ps.tile([P, 2, 2, P], F32, name=f"even{h}")
             yz[h, 0], yz[h, 2] = even[:, 0], even[:, 1]
             for d in (1, 3):
@@ -83,8 +87,8 @@ def tile_picked_yarap_rhs_p_kernel(
 
         x_picked, x_codes, w_codes, w_scales = {}, {}, {}, {}
 
-        def gather_words(o, tag=None):
-            x_picked[o] = tile([P, S], U32, f"x_picked{o}", tag)
+        def gather_words(o, after=None):
+            x_picked[o] = tile([P, S], U32, f"x_picked{o}", after)
             nc.vector.tensor_copy(x_picked[o][:], x_table[o][:].indirect(offsets[:]))
 
         def deal(src, dtype, name, run):
@@ -96,11 +100,12 @@ def tile_picked_yarap_rhs_p_kernel(
             return dst
 
         def cast(dst, piece, copy):
-            copy(dst.rearrange("p (g i) t -> p g t i", i=4), w_raw[piece].rearrange("p t (g i) -> p g t i", i=4))
+            run = LINE // 4
+            copy(dst.rearrange("p (g i) t -> p g t i", i=run), w_raw[piece].rearrange("p t (g i) -> p g t i", i=run))
 
-        def mx_tiles(o, h, codes_tag=None, scales_tag=None):
-            w_codes[o, h] = tile([P, 2 * P], U32, f"w_codes{o}{h}", codes_tag)
-            w_scales[o, h] = tile([P, 2 * P], U8, f"w_scales{o}{h}", scales_tag)
+        def mx_tiles(o, h, codes_after=None, scales_after=None):
+            w_codes[o, h] = tile([P, 2 * P], U32, f"w_codes{o}{h}", codes_after)
+            w_scales[o, h] = tile([P, 2 * P], U8, f"w_scales{o}{h}", scales_after)
 
         def quantise(o, h, cols, src):
             nc.vector.quantize_mx(out=w_codes[o, h][:, cols].bitcast(FP8X4), scales=w_scales[o, h][:, cols], in_=src)
@@ -111,7 +116,7 @@ def tile_picked_yarap_rhs_p_kernel(
                 nc.tensor.matmul_mx(
                     out=yz[h, d].rearrange("p c m -> p (c m)"),
                     lhsT=x_codes[o][:, cols].bitcast(FP8X4),
-                    lhsT_scale=s_dealt[4 * o :, cols],
+                    lhsT_scale=s_dealt[PACK * o :, cols],
                     rhs=w_codes[o, h][:].bitcast(FP8X4),
                     rhs_scale=w_scales[o, h][:],
                     start=(o == 0 and d != 2),
@@ -121,74 +126,64 @@ def tile_picked_yarap_rhs_p_kernel(
         gather_words(0)
         s_picked = tile([P, S], U8, "s_picked")
         nc.vector.tensor_copy(s_picked[:], s_table[:].indirect(offsets[:]))
-        x_codes[0] = deal(x_picked[0], U32, "x_codes0", 4)
-        s_dealt = deal(s_picked, U8, "s_dealt", 16)
-        first_bf = [tile([P, 2, P, PACK], BF16, f"w_bf0{h}") for h in range(BLOCKS)]
+        x_codes[0] = deal(x_picked[0], U32, "x_codes0", LINE // 4)
+        s_dealt = deal(s_picked, U8, "s_dealt", LINE)
+        first_bf = [tile([P, 2, P, PACK], BF16, f"w_bf0{h}") for h in range(HALVES)]
         for c in range(2):
-            for h in range(BLOCKS):
+            for h in range(HALVES):
                 cast(first_bf[h][:, c], (0, h, c), nc.scalar.copy)
-        for h in range(BLOCKS):
+        for h in range(HALVES):
             mx_tiles(0, h)
             quantise(0, h, slice(0, 2 * P), first_bf[h][:].rearrange("p c m t -> p (c m t)"))
             products(0, h)
 
-        factors = tile([P, 4, D], F32, "factors", "w_raw01")
+        factors = tile([P, 4, D], F32, "factors", after="w_raw01")
         sums = tile([P, 2], F32, "sums")
-        a, b, nb = factors[:, 0, :], factors[:, 1, :], factors[:, 2, :]
+        a, b, minus_b, a_again = (factors[:, row, :] for row in range(4))
         for d in range(D):
             nc.scalar.activation(factors[:, 0:2, d], rest[:, :, d], ACT.Copy, scale=cot_t[:, d : d + 1])
-        nc.scalar.activation(factors[:, 3, :], a, ACT.Copy, accum_out=sums[:, 0:1])
-        nc.scalar.activation(nb, b, ACT.Copy, scale=-1.0, accum_out=sums[:, 1:2])
+        nc.scalar.activation(a_again, a, ACT.Copy, accum_out=sums[:, 0:1])
+        nc.scalar.activation(minus_b, b, ACT.Copy, scale=-1.0, accum_out=sums[:, 1:2])
         spread_ps = ps.tile([P, 2, V], F32, name="spread_ps")
         for i in range(2):
             nc.tensor.transpose(spread_ps[:, i, :], sums[:, i : i + 1].to_broadcast([P, P]), ident[:])
-        spread = tile([P, 2, V], F32, "spread")
+
+        gather_words(1, after="w_bf01")
+        x_codes[1] = deal(x_picked[1], U32, "x_codes1", LINE // 4)
+        half0_bf = tile([P, 2, P, PACK], BF16, "w_bf10", after="rest")
+        for c in range(2):
+            cast(half0_bf[:, c], (1, 0, c), nc.scalar.copy)
+        mx_tiles(1, 0, codes_after="x_table1")
+        quantise(1, 0, slice(0, 2 * P), half0_bf[:].rearrange("p c m t -> p (c m t)"))
+        products(1, 0)
+        half1_bf = [tile([P, P, PACK], BF16, "w_bf110"), tile([P, P, PACK], BF16, "w_bf111", after="rest")]
+        mx_tiles(1, 1, scales_after="w_bf01")
+        for c, copy in ((1, nc.vector.tensor_copy), (0, nc.scalar.copy)):
+            cast(half1_bf[c][:], (1, 1, c), copy)
+        for c in range(2):
+            quantise(1, 1, slice(c * P, (c + 1) * P), half1_bf[c][:].rearrange("p m t -> p (m t)"))
+        products(1, 1)
+        spread = tile([P, 2, V], F32, "spread", after="w_raw110")
         nc.scalar.copy(spread[:], spread_ps[:])
 
-        gather_words(1, "w_bf01")
-        warm_ps = ps.tile([P, 2 * P], F32, name="warm_ps")
-        for d in range(D):
-            cols = slice(d * V, (d + 1) * V)
-            nc.tensor.matmul_mx(
-                out=warm_ps[:],
-                lhsT=x_picked[1][:, cols].bitcast(FP8X4),
-                lhsT_scale=s_picked[4:, cols],
-                rhs=w_codes[0, 1][:].bitcast(FP8X4),
-                rhs_scale=w_scales[0, 1][:],
-                start=True,
-                stop=True,
-            )
-        x_codes[1] = deal(x_picked[1], U32, "x_codes1", 4)
-        block0_bf = tile([P, 2, P, PACK], BF16, "w_bf10", "w_bf00")
-        for c in range(2):
-            cast(block0_bf[:, c], (1, 0, c), nc.scalar.copy)
-        mx_tiles(1, 0, codes_tag="x_table1")
-        quantise(1, 0, slice(0, 2 * P), block0_bf[:].rearrange("p c m t -> p (c m t)"))
-        products(1, 0)
-        halves = [tile([P, P, PACK], BF16, "w_bf110"), tile([P, P, PACK], BF16, "w_bf111", "w_bf00")]
-        mx_tiles(1, 1, scales_tag="w_bf01")
-        for c, copy in ((1, nc.vector.tensor_copy), (0, nc.scalar.copy)):
-            cast(halves[c][:], (1, 1, c), copy)
-        for c in range(2):
-            quantise(1, 1, slice(c * P, (c + 1) * P), halves[c][:].rearrange("p m t -> p (m t)"))
-        products(1, 1)
-
-        acc0 = ps.tile([P, 2, V], F32, name="acc0", tag="warm_ps")
+        acc0 = ps.tile([P, 2, V], F32, name="acc0")
         acc = {(0, 0): acc0[:, 0], (0, 1): acc0[:, 1]}
-        for h in range(BLOCKS):
-            names = ("a0", "b0", "b2", "a3", "a2", "a1", "b1", "b3")
-            t = {n: tile([P, 2, P], F32, f"{n}_{h}", "w_bf00" if (n, h) == ("a1", 0) else None) for n in names}
-            for n in names[:5]:
+        for h in range(HALVES):
+            plain, adding = ("a0", "b0", "b2", "a3", "a2"), ("a1", "b1", "b3")
+            term = {n: tile([P, 2, P], F32, f"{n}_{h}", "rest" if (n, h) == ("a1", 0) else None) for n in plain + adding}
+            for n in plain:
                 d = int(n[1])
+                factor = (a if n[0] == "a" else b)[:, d : d + 1]
                 if (n, h) == ("a3", 1):
-                    nc.vector.tensor_scalar(t[n][:], yz[h, d], a[:, d : d + 1], None, ALU.mult)
+                    nc.vector.tensor_scalar(term[n][:], yz[h, d], factor, None, ALU.mult)
                 else:
-                    nc.scalar.activation(t[n][:], yz[h, d], ACT.Copy, scale=(a if n[0] == "a" else b)[:, d : d + 1])
-            nc.vector.scalar_tensor_tensor(t["a1"][:], yz[h, 1], a[:, 1:2], t["a0"][:], ALU.mult, ALU.add)
+                    nc.scalar.activation(term[n][:], yz[h, d], ACT.Copy, scale=factor)
+            nc.vector.scalar_tensor_tensor(term["a1"][:], yz[h, 1], a[:, 1:2], term["a0"][:], ALU.mult, ALU.add)
             for d in (1, 3):
-                new, old = t[f"b{d}"], t[f"b{d - 1}"]
-                nc.vector.scalar_tensor_tensor(new[:, 0], yz[h, d][:, 1], b[:, d : d + 1], old[:, 1], ALU.mult, ALU.add)
-                nc.vector.scalar_tensor_tensor(new[:, 1], yz[h, d][:, 0], nb[:, d : d + 1], old[:, 0], ALU.mult, ALU.subtract)
+                new, old = term[f"b{d}"], term[f"b{d - 1}"]
+                y, z = yz[h, d][:, 0], yz[h, d][:, 1]
+                nc.vector.scalar_tensor_tensor(new[:, 0], z, b[:, d : d + 1], old[:, 1], ALU.mult, ALU.add)
+                nc.vector.scalar_tensor_tensor(new[:, 1], y, minus_b[:, d : d + 1], old[:, 0], ALU.mult, ALU.subtract)
             if h == 1:
                 acc[1, 0] = ps.tile([P, V], F32, name="acc10", tag="even0")[:]
                 acc[1, 1] = ps.tile([P, V], F32, name="acc11", tag="spread_ps")[:]
@@ -197,26 +192,26 @@ def tile_picked_yarap_rhs_p_kernel(
                 for i in range(2):
                     first = n == order[0] and (h == 1 or i == 0)
                     last = n == order[-1] and (h == 1 or i == 1)
-                    nc.tensor.matmul(acc[h, i], t[n][:, i], ident[:], is_transpose=True, start=first, stop=last)
+                    nc.tensor.matmul(acc[h, i], term[n][:, i], ident[:], is_transpose=True, start=first, stop=last)
 
-        squares = [tile([P, 2, V], F32, f"squares{h}") for h in range(BLOCKS)]
-        scaled = [tile([P, 2, V], F32, f"scaled{h}") for h in range(BLOCKS)]
-        norm2 = [tile([P, V], F32, f"norm2{h}") for h in range(BLOCKS)]
-        num = [tile([P, V], F32, f"num{h}") for h in range(BLOCKS)]
-        inv = [tile([P, V], F32, "inv0", "b3_1"), tile([P, V], F32, "inv1")]
-        res = [tile([P, V], F32, f"res{h}") for h in range(BLOCKS)]
+        squares = [tile([P, 2, V], F32, f"squares{h}") for h in range(HALVES)]
+        scaled = [tile([P, 2, V], F32, f"scaled{h}") for h in range(HALVES)]
+        norm2 = [tile([P, V], F32, f"norm2{h}") for h in range(HALVES)]
+        numerator = [tile([P, V], F32, f"numerator{h}") for h in range(HALVES)]
+        inverse = [tile([P, V], F32, "inverse0", after="b3_1"), tile([P, V], F32, "inverse1")]
+        result = [tile([P, V], F32, f"result{h}") for h in range(HALVES)]
         nc.scalar.activation(squares[0][:], acc0[:], ACT.Square)
         for i in range(2):
             nc.scalar.activation(squares[1][:, i], acc[1, i], ACT.Square)
         nc.vector.tensor_tensor(norm2[0][:], squares[0][:, 0], squares[0][:, 1], ALU.add)
         nc.vector.tensor_tensor(scaled[0][:], acc0[:], spread[:], ALU.mult)
         nc.vector.tensor_tensor(scaled[1][:, 0], acc[1, 0], spread[:, 0], ALU.mult)
-        nc.vector.tensor_tensor(num[0][:], scaled[0][:, 0], scaled[0][:, 1], ALU.add)
+        nc.vector.tensor_tensor(numerator[0][:], scaled[0][:, 0], scaled[0][:, 1], ALU.add)
         nc.vector.tensor_tensor(norm2[1][:], squares[1][:, 0], squares[1][:, 1], ALU.add)
         nc.vector.tensor_tensor(scaled[1][:, 1], acc[1, 1], spread[:, 1], ALU.mult)
-        for h in range(BLOCKS):
-            nc.scalar.activation(inv[h][:], norm2[h][:], ACT.Abs_reciprocal_sqrt, bias=0.1)
-        nc.vector.tensor_tensor(num[1][:], scaled[1][:, 0], scaled[1][:, 1], ALU.add)
-        for h in range(BLOCKS):
-            nc.vector.tensor_tensor(res[h][:], num[h][:], inv[h][:], ALU.mult)
-            nc.sync.dma_start(out=out[h * P : (h + 1) * P, :], in_=res[h][:])
+        for h in range(HALVES):
+            nc.scalar.activation(inverse[h][:], norm2[h][:], ACT.Abs_reciprocal_sqrt, bias=EPSILON)
+        nc.vector.tensor_tensor(numerator[1][:], scaled[1][:, 0], scaled[1][:, 1], ALU.add)
+        for h in range(HALVES):
+            nc.vector.tensor_tensor(result[h][:], numerator[h][:], inverse[h][:], ALU.mult)
+            nc.sync.dma_start(out=out[h * P : (h + 1) * P, :], in_=result[h][:])

from contextlib import ExitStack

import concourse.mybir as mybir
from concourse.masks import make_identity

K, T, S, D, N = 1024, 2048, 512, 4, 256
FLOPS = 2 * 2 * K * N * S

F32 = mybir.dt.float32
BF16 = mybir.dt.bfloat16
I32 = mybir.dt.int32
U32 = mybir.dt.uint32
U16 = mybir.dt.uint16
U8 = mybir.dt.uint8
FP8X4 = mybir.dt.float8_e4m3fn_x4
ACT = mybir.ActivationFunctionType
ALU = mybir.AluOpType

P = 128
PACK = 4
PASSES = K // (P * PACK)
V = S // D
HALVES = N // P
QUADRANTS = 4
LINE = 16
EPSILON = 0.1


def tile_picked_yarap_rhs_p_kernel(
    tc, x_words, x_scales, w1, w2, cot, rx, ry, offs, out
):
    nc = tc.nc
    weights = (w1, w2)
    with ExitStack() as ctx:
        sb = ctx.enter_context(tc.tile_pool(name="sb", bufs=1))
        ps = ctx.enter_context(tc.psum_pool(name="ps", bufs=1))

        def tile(shape, dtype, name, after=None):
            return sb.tile(shape, dtype, name=name, tag=after or name, align_bytes=64)

        offsets = sb.tile([P, S // 16], U16, name="offsets")
        x_table = [tile([P, T], U32, f"x_table{o}") for o in range(PASSES)]
        s_table = tile([P, T], U8, "s_table")
        first_raw = [tile([P, PACK, N], F32, f"w_raw0{c}") for c in range(2)]
        last_raw = {(h, c): tile([P, PACK, P], F32, f"w_raw1{h}{c}") for h in range(HALVES) for c in range(2)}
        w_raw = {(0, h, c): first_raw[c][:, :, h * P : (h + 1) * P] for h in range(HALVES) for c in range(2)}
        w_raw.update({(1, h, c): last_raw[h, c][:] for h, c in last_raw})
        cot_t = tile([P, D], F32, "cot_t")
        rest = tile([P, 2, 2 * D], F32, "rest")
        ident = tile([P, P], F32, "ident")

        def load_x(o):
            nc.sync.dma_start(out=x_table[o][:].bitcast(I32), in_=x_words[o].rearrange("p n t -> p (n t)").bitcast(I32))

        def load_w(dst, o, c, cols):
            rows = weights[c][o * P * PACK : (o + 1) * P * PACK, cols]
            nc.sync.dma_start(out=dst[:], in_=rows.rearrange("(p t) m -> p t m", t=PACK))

        nc.vector.memset(s_table[:].bitcast(I32), 0)
        load_x(0)
        nc.sync.dma_start(offsets[:], offs)
        for q in range(QUADRANTS):
            nc.sync.dma_start(
                out=s_table[32 * q : 32 * q + PACK * PASSES, :].bitcast(I32),
                in_=x_scales[:, PACK * q : PACK * (q + 1), :].bitcast(I32),
            )
        for c in range(2):
            load_w(first_raw[c], 0, c, slice(0, N))
        for dst, rows in ((cot_t[:], cot), (rest[:, 0, 0:D], rx), (rest[:, 1, 0:D], ry)):
            nc.sync.dma_start(out=dst, in_=rows[0].rearrange("(v d) -> v d", d=D))
        load_x(1)
        for h, c in last_raw:
            load_w(last_raw[h, c], 1, c, slice(h * P, (h + 1) * P))

        warm = tile([P, 2], F32, "warm")
        nc.gpsimd.memset(warm[:, 0:1], 1.0)
        nc.scalar.activation(warm[:, 1:2], warm[:, 0:1], ACT.Abs_reciprocal_sqrt, bias=EPSILON)

        make_identity(nc, ident[:])

        yz = {}
        for h in range(HALVES):
            even = ps.tile([P, 2, 2, P], F32, name=f"even{h}")
            yz[h, 0], yz[h, 2] = even[:, 0], even[:, 1]
            for d in (1, 3):
                yz[h, d] = ps.tile([P, 2, P], F32, name=f"odd{h}{d}")[:]

        x_picked, x_codes, w_codes, w_scales = {}, {}, {}, {}

        def gather_words(o, after=None):
            x_picked[o] = tile([P, S], U32, f"x_picked{o}", after)
            nc.vector.tensor_copy(x_picked[o][:], x_table[o][:].indirect(offsets[:]))

        def deal(src, dtype, name, run):
            dst = tile([P, S], dtype, name)
            nc.vector.tensor_copy(
                dst[:].rearrange("p (d g i) -> p g d i", d=D, i=run),
                src[:].rearrange("p (g i d) -> p g d i", d=D, i=run),
            )
            return dst

        def cast(dst, piece, copy):
            run = LINE // 4
            copy(dst.rearrange("p (g i) t -> p g t i", i=run), w_raw[piece].rearrange("p t (g i) -> p g t i", i=run))

        def mx_tiles(o, h, codes_after=None, scales_after=None):
            w_codes[o, h] = tile([P, 2 * P], U32, f"w_codes{o}{h}", codes_after)
            w_scales[o, h] = tile([P, 2 * P], U8, f"w_scales{o}{h}", scales_after)

        def quantise(o, h, cols, src):
            nc.vector.quantize_mx(out=w_codes[o, h][:, cols].bitcast(FP8X4), scales=w_scales[o, h][:, cols], in_=src)

        def products(o, h):
            for d in (0, 2, 3, 1):
                cols = slice(d * V, (d + 1) * V)
                nc.tensor.matmul_mx(
                    out=yz[h, d].rearrange("p c m -> p (c m)"),
                    lhsT=x_codes[o][:, cols].bitcast(FP8X4),
                    lhsT_scale=s_dealt[PACK * o :, cols],
                    rhs=w_codes[o, h][:].bitcast(FP8X4),
                    rhs_scale=w_scales[o, h][:],
                    start=(o == 0 and d != 2),
                    stop=(o == PASSES - 1 and d != 0),
                )

        gather_words(0)
        s_picked = tile([P, S], U8, "s_picked")
        nc.vector.tensor_copy(s_picked[:], s_table[:].indirect(offsets[:]))
        x_codes[0] = deal(x_picked[0], U32, "x_codes0", LINE // 4)
        s_dealt = deal(s_picked, U8, "s_dealt", LINE)
        first_bf = [tile([P, 2, P, PACK], BF16, f"w_bf0{h}") for h in range(HALVES)]
        for c in range(2):
            for h in range(HALVES):
                cast(first_bf[h][:, c], (0, h, c), nc.scalar.copy)
        for h in range(HALVES):
            mx_tiles(0, h)
            quantise(0, h, slice(0, 2 * P), first_bf[h][:].rearrange("p c m t -> p (c m t)"))
            products(0, h)

        factors = tile([P, 4, D], F32, "factors", after="w_raw01")
        sums = tile([P, 2], F32, "sums")
        a, b, minus_b, a_again = (factors[:, row, :] for row in range(4))
        for d in range(D):
            nc.scalar.activation(factors[:, 0:2, d], rest[:, :, d], ACT.Copy, scale=cot_t[:, d : d + 1])
        nc.scalar.activation(a_again, a, ACT.Copy, accum_out=sums[:, 0:1])
        nc.scalar.activation(minus_b, b, ACT.Copy, scale=-1.0, accum_out=sums[:, 1:2])
        spread_ps = ps.tile([P, 2, V], F32, name="spread_ps")
        for i in range(2):
            nc.tensor.transpose(spread_ps[:, i, :], sums[:, i : i + 1].to_broadcast([P, P]), ident[:])

        gather_words(1, after="w_bf01")
        x_codes[1] = deal(x_picked[1], U32, "x_codes1", LINE // 4)
        half0_bf = tile([P, 2, P, PACK], BF16, "w_bf10", after="rest")
        for c in range(2):
            cast(half0_bf[:, c], (1, 0, c), nc.scalar.copy)
        mx_tiles(1, 0, codes_after="x_table1")
        quantise(1, 0, slice(0, 2 * P), half0_bf[:].rearrange("p c m t -> p (c m t)"))
        products(1, 0)
        half1_bf = [tile([P, P, PACK], BF16, "w_bf110"), tile([P, P, PACK], BF16, "w_bf111", after="rest")]
        mx_tiles(1, 1, scales_after="w_bf01")
        for c, copy in ((1, nc.vector.tensor_copy), (0, nc.scalar.copy)):
            cast(half1_bf[c][:], (1, 1, c), copy)
        for c in range(2):
            quantise(1, 1, slice(c * P, (c + 1) * P), half1_bf[c][:].rearrange("p m t -> p (m t)"))
        products(1, 1)
        spread = tile([P, 2, V], F32, "spread", after="w_raw110")
        nc.scalar.copy(spread[:], spread_ps[:])

        acc0 = ps.tile([P, 2, V], F32, name="acc0")
        acc = {(0, 0): acc0[:, 0], (0, 1): acc0[:, 1]}
        for h in range(HALVES):
            plain, adding = ("a0", "b0", "b2", "a3", "a2"), ("a1", "b1", "b3")
            term = {n: tile([P, 2, P], F32, f"{n}_{h}", "rest" if (n, h) == ("a1", 0) else None) for n in plain + adding}
            for n in plain:
                d = int(n[1])
                factor = (a if n[0] == "a" else b)[:, d : d + 1]
                if (n, h) == ("a3", 1):
                    nc.vector.tensor_scalar(term[n][:], yz[h, d], factor, None, ALU.mult)
                else:
                    nc.scalar.activation(term[n][:], yz[h, d], ACT.Copy, scale=factor)
            nc.vector.scalar_tensor_tensor(term["a1"][:], yz[h, 1], a[:, 1:2], term["a0"][:], ALU.mult, ALU.add)
            for d in (1, 3):
                new, old = term[f"b{d}"], term[f"b{d - 1}"]
                y, z = yz[h, d][:, 0], yz[h, d][:, 1]
                nc.vector.scalar_tensor_tensor(new[:, 0], z, b[:, d : d + 1], old[:, 1], ALU.mult, ALU.add)
                nc.vector.scalar_tensor_tensor(new[:, 1], y, minus_b[:, d : d + 1], old[:, 0], ALU.mult, ALU.subtract)
            if h == 1:
                acc[1, 0] = ps.tile([P, V], F32, name="acc10", tag="even0")[:]
                acc[1, 1] = ps.tile([P, V], F32, name="acc11", tag="spread_ps")[:]
            order = (("a1", "a3", "a2", "b1", "b3"), ("a3", "a1", "b1", "a2", "b3"))[h]
            for n in order:
                for i in range(2):
                    first = n == order[0] and (h == 1 or i == 0)
                    last = n == order[-1] and (h == 1 or i == 1)
                    nc.tensor.matmul(acc[h, i], term[n][:, i], ident[:], is_transpose=True, start=first, stop=last)

        squares = [tile([P, 2, V], F32, f"squares{h}") for h in range(HALVES)]
        scaled = [tile([P, 2, V], F32, f"scaled{h}") for h in range(HALVES)]
        norm2 = [tile([P, V], F32, f"norm2{h}") for h in range(HALVES)]
        numerator = [tile([P, V], F32, f"numerator{h}") for h in range(HALVES)]
        inverse = [tile([P, V], F32, "inverse0", after="b3_1"), tile([P, V], F32, "inverse1")]
        result = [tile([P, V], F32, f"result{h}") for h in range(HALVES)]
        nc.scalar.activation(squares[0][:], acc0[:], ACT.Square)
        for i in range(2):
            nc.scalar.activation(squares[1][:, i], acc[1, i], ACT.Square)
        nc.vector.tensor_tensor(norm2[0][:], squares[0][:, 0], squares[0][:, 1], ALU.add)
        nc.vector.tensor_tensor(scaled[0][:], acc0[:], spread[:], ALU.mult)
        nc.vector.tensor_tensor(scaled[1][:, 0], acc[1, 0], spread[:, 0], ALU.mult)
        nc.vector.tensor_tensor(numerator[0][:], scaled[0][:, 0], scaled[0][:, 1], ALU.add)
        nc.vector.tensor_tensor(norm2[1][:], squares[1][:, 0], squares[1][:, 1], ALU.add)
        nc.vector.tensor_tensor(scaled[1][:, 1], acc[1, 1], spread[:, 1], ALU.mult)
        for h in range(HALVES):
            nc.scalar.activation(inverse[h][:], norm2[h][:], ACT.Abs_reciprocal_sqrt, bias=EPSILON)
        nc.vector.tensor_tensor(numerator[1][:], scaled[1][:, 0], scaled[1][:, 1], ALU.add)
        for h in range(HALVES):
            nc.vector.tensor_tensor(result[h][:], numerator[h][:], inverse[h][:], ALU.mult)
            nc.sync.dma_start(out=out[h * P : (h + 1) * P, :], in_=result[h][:])
